import numpy as np
import ml_dtypes


def mxq(x, axis, fmt="e4m3"):
    dtype, down = {"e4m3": (ml_dtypes.float8_e4m3fn, 7), "e5m2": (ml_dtypes.float8_e5m2, 14)}[fmt]
    v = np.moveaxis(np.asarray(x, np.float32).astype(ml_dtypes.bfloat16).astype(np.float64), axis, -1)
    blocks = v.reshape(v.shape[:-1] + (-1, 32))
    amax = np.abs(blocks).max(-1, keepdims=True)
    byte = np.maximum(np.where(amax > 0, np.frexp(amax)[1] - 1 + 127, 0) - down, 1)
    scale = np.exp2(byte - 127.0)
    codes = (blocks / scale).astype(np.float32).astype(dtype).astype(np.float64)
    return np.moveaxis((codes * scale).reshape(v.shape), -1, axis)


WIDE = False


def mx_kscale(k):
    if not WIDE:
        return np.ones(k)
    levels = np.array([10, -10, 5, -5, 0])
    if k % 512:
        return np.exp2(np.random.permutation(np.resize(levels, k // 32))).repeat(32)
    a = np.empty((k // 512, 16))
    for p in range(k // 512):
        a[p, :8] = np.random.permutation(np.resize(levels, 8))
        for g in range(8):
            far = levels[np.abs(levels - a[p, g]) >= 10]
            a[p, g + 8] = far[np.random.randint(len(far))]
    return np.exp2(a.ravel()).repeat(32)


def f64(x):
    return np.asarray(x).astype(np.float64)


def striped(idx):
    return np.tile(np.asarray(idx).reshape(-1, 16).T, (8, 1)).astype(np.uint16)


def unstriped(offs):
    return offs[:16].T.reshape(-1).astype(np.int64)


E2M1 = np.array([0.0, 0.5, 1.0, 1.5, 2.0, 3.0, 4.0, 6.0, -0.0, -0.5, -1.0, -1.5, -2.0, -3.0, -4.0, -6.0])


def pack_weight(w, fmt):
    k, n = w.shape
    w = f64(np.asarray(w, np.float32).astype(ml_dtypes.bfloat16)).reshape(k // 32, 32, n)
    amax = np.abs(w).max(1)
    if fmt == "e4m3":
        byte = np.frexp(amax)[1] - 1 + 127 - 7
    else:
        mant, ex = np.frexp(amax / 6.0)
        byte = np.where(mant > 0.5, ex, ex - 1) + 127
    byte = np.clip(np.where(amax > 0, byte, 1), 1, 254)
    scaled = (w * np.exp2(127.0 - byte)[:, None, :]).reshape(k, n).astype(np.float32)
    by_word = np.ascontiguousarray(scaled.reshape(k // 512, 128, 4, n).transpose(0, 1, 3, 2))
    if fmt == "e4m3":
        words = by_word.astype(ml_dtypes.float8_e4m3fn).view(np.uint8)
    else:
        c = by_word.astype(ml_dtypes.float4_e2m1fn).view(np.uint8) & 0xF
        words = (c[..., 0::2] | (c[..., 1::2] << 4)).reshape(k // 512, 128, 2 * n)
    return np.ascontiguousarray(words), np.ascontiguousarray(byte.astype(np.uint8).reshape(k // 512, 16, n))


def unpack_weight(words, scales, fmt):
    g, _, n = scales.shape
    words = np.ascontiguousarray(words).reshape(g, 128, n, -1)
    if fmt == "e4m3":
        vals = words.view(ml_dtypes.float8_e4m3fn).astype(np.float64)
    else:
        nib = np.empty((g, 128, n, 4), np.uint8)
        nib[..., 0::2] = words & 0xF
        nib[..., 1::2] = words >> 4
        vals = E2M1[nib]
    vals = vals * np.repeat(np.exp2(scales.astype(np.float64) - 127.0), 8, axis=1)[..., None]
    return vals.transpose(0, 1, 3, 2).reshape(g * 512, n)


def sigmoid(v):
    return 1.0 / (1.0 + np.exp(-v))


D, T, I, Q, E, M = 512, 2048, 512, 128, 512, 512


def setup_inputs():
    n = np.random.standard_normal
    idx = np.random.permutation(T)[:I]
    fd = mx_kscale(D)
    fm = mx_kscale(M)
    fi = mx_kscale(I)
    ti = np.ones(T)
    ti[idx] = fi
    keysp = pack_weight(n((D, T)) / fd[:, None], "e4m3")
    return {
        "query": (n((D, Q)) * 0.4 / np.sqrt(D) * fd[:, None]).astype(np.float32),
        "wkey": (n((D, M)) / fd[:, None]).astype(np.float32),
        "wval": (n((M, E)) / fm[:, None]).astype(np.float32),
        "keys_words": keysp[0],
        "keys_scales": keysp[1],
        "vals": (n((E, T)) / ti).astype(np.float32),
        "th": (np.random.uniform(0.8, 1.6, (Q, 1))).astype(np.float32),
        "steep": (np.random.uniform(1.0, 3.0, (Q, 1))).astype(np.float32),
        "wf": (np.random.uniform(0.5, 2.0, (1, M)) * fm).astype(np.float32),
        "size": (np.random.uniform(0.5, 2.0, (1, I)) * fi).astype(np.float32),
        "offs": striped(idx),
    }


def reference(query, wkey, wval, keys_words, keys_scales, vals, th, steep, wf, size, offs):
    idx = unstriped(offs)
    keysu = unpack_weight(keys_words, keys_scales, "e4m3")
    queryq = mxq(f64(query), 0, "e4m3")
    wkeyq = mxq(f64(wkey), 0, "e4m3")
    a = queryq.T @ wkeyq
    keysidxg = keysu[:, idx]
    b = queryq.T @ keysidxg
    z = np.max(b, axis=1, keepdims=True)
    g = sigmoid(f64(steep) * (z - f64(th)))
    p = np.exp(a - np.max(a, axis=1, keepdims=True))
    w = p * f64(wf) * (1.0 - g) / np.sum(p, axis=1, keepdims=True)
    wt = w.T
    r = np.exp(b - z)
    u = r * f64(size) * g / np.sum(r, axis=1, keepdims=True)
    ut = u.T
    vt = f64(vals)[:, idx].T
    wtq = mxq(wt, 0, "e4m3")
    wvalq = mxq(f64(wval), 0, "e4m3")
    utq = mxq(ut, 0, "e4m3")
    vtq = mxq(vt, 0, "e4m3")
    o = wtq.T @ wvalq + utq.T @ vtq
    return o

@@ -1,0 +1,218 @@
+from contextlib import ExitStack
+
+import concourse.mybir as mybir
+from concourse.masks import make_identity
+
+D, T, I, Q, E, M = 512, 2048, 512, 128, 512, 512
+FLOPS = 2 * Q * (D * M + D * I + M * E + I * E)
+
+F32 = mybir.dt.float32
+BF16 = mybir.dt.bfloat16
+I32 = mybir.dt.int32
+U32 = mybir.dt.uint32
+U16 = mybir.dt.uint16
+U8 = mybir.dt.uint8
+FP8X4 = mybir.dt.float8_e4m3fn_x4
+ALU = mybir.AluOpType
+ACT = mybir.ActivationFunctionType
+AX = mybir.AxisListType
+
+P = 128
+PACK = 4
+BLOCKS = E // P
+WKEY_SPLIT = 256
+GATHER_SPLIT = 288
+WVAL_LOADS = ((2, 3), (1,), (0,))
+
+
+def tile_attend_confidencegate_kernel(
+    tc, query, wkey, wval, keys_words, keys_scales, vals, th, steep, wf, size, offs, out
+):
+    nc = tc.nc
+    with ExitStack() as ctx:
+        sb = ctx.enter_context(tc.tile_pool(name="sb", bufs=1))
+        ps = ctx.enter_context(tc.psum_pool(name="ps", bufs=1))
+
+        def tile(name, shape, dtype, tag=None):
+            return sb.tile(shape, dtype, name=name, tag=tag or name, align_bytes=64)
+
+        def quantize(name, grouped, width):
+            codes = tile(name + "_codes", [P, width], U32)
+            scales = tile(name + "_scales", [P, width], U8)
+            nc.vector.quantize_mx(out=codes[:].bitcast(FP8X4), scales=scales[:], in_=grouped)
+            return codes, scales
+
+        def product(acc, lhs, rhs, cols, start, stop):
+            nc.tensor.matmul_mx(
+                out=acc,
+                lhsT=lhs[0][:].bitcast(FP8X4),
+                lhsT_scale=lhs[1][:],
+                rhs=rhs[0][:, cols].bitcast(FP8X4),
+                rhs_scale=rhs[1][:, cols],
+                start=start,
+                stop=stop,
+            )
+
+        query_raw = tile("query_raw", [P, PACK, Q], F32)
+        nc.sync.dma_start(out=query_raw[:], in_=query.rearrange("(p j) q -> p j q", j=PACK))
+        scale_rows = tile("scale_rows", [P, T // 4], I32)
+        for quad in range(4):
+            nc.sync.dma_start(
+                out=scale_rows[32 * quad : 32 * quad + 4, :],
+                in_=keys_scales[0, 4 * quad : 4 * quad + 4, :].bitcast(I32),
+            )
+        offsets = sb.tile([P, I // 16], U16, name="offsets")
+        nc.sync.dma_start(offsets[:], offs)
+        wkey_raw = tile("wkey_raw", [P, PACK, M], F32)
+        nc.sync.dma_start(out=wkey_raw[:], in_=wkey.rearrange("(p j) m -> p j m", j=PACK))
+        key_words = tile("key_words", [P, T], U32)
+        nc.sync.dma_start(
+            out=key_words[:].bitcast(I32),
+            in_=keys_words[0].rearrange("p n t -> p (n t)").bitcast(I32),
+        )
+        th_col = tile("th_col", [P, 1], F32)
+        nc.sync.dma_start(out=th_col[:], in_=th)
+        steep_col = tile("steep_col", [P, 1], F32)
+        nc.sync.dma_start(out=steep_col[:], in_=steep)
+        vals_raw = [tile("vals_raw%d" % j, [P, T], F32) for j in range(BLOCKS)]
+        nc.sync.dma_start(out=vals_raw[0][:], in_=vals[:P, :])
+        size4 = tile("size4", [P, PACK], F32)
+        nc.sync.dma_start(out=size4[:], in_=size.rearrange("o (p r) -> (o p) r", r=PACK))
+        wf4 = tile("wf4", [P, PACK], F32)
+        nc.sync.dma_start(out=wf4[:], in_=wf.rearrange("o (p r) -> (o p) r", r=PACK))
+        for j in range(1, BLOCKS):
+            nc.sync.dma_start(out=vals_raw[j][:], in_=vals[j * P : (j + 1) * P, :])
+        wval_rows = wval.rearrange("(p j) e -> p j e", j=PACK)
+        wval_raw = []
+        for n, blocks in enumerate(WVAL_LOADS):
+            raw = tile("wval_raw%d" % n, [P, PACK, P * len(blocks)], F32)
+            nc.sync.dma_start(out=raw[:], in_=wval_rows[:, :, blocks[0] * P : (blocks[-1] + 1) * P])
+            wval_raw.append(raw)
+
+        ident = tile("ident", [P, P], F32)
+        make_identity(nc, ident[:])
+
+        query_bf = tile("query_bf", [P, Q, PACK], BF16)
+        nc.scalar.activation(out=query_bf[:], in_=query_raw[:].rearrange("p j q -> p q j"), func=ACT.Copy)
+        key_bytes = tile("key_bytes", [P, T], U8)
+        nc.vector.memset(key_bytes[:].bitcast(I32), 0)
+        for quad in range(4):
+            rows = slice(32 * quad, 32 * quad + 4)
+            nc.vector.tensor_copy(out=key_bytes[rows, :].bitcast(I32), in_=scale_rows[rows, :])
+        query_mx = quantize("query", query_bf[:].rearrange("p q j -> p (q j)"), Q)
+        got_bytes = tile("got_bytes", [P, I], U8)
+        nc.vector.tensor_copy(out=got_bytes[:], in_=key_bytes[:].indirect(offsets[:]))
+        wkey_bf = tile("wkey_bf", [P, M, PACK], BF16)
+        wkey_stepped = wkey_raw[:].rearrange("p j m -> p m j")
+        nc.vector.tensor_copy(out=wkey_bf[:, :WKEY_SPLIT, :], in_=wkey_stepped[:, :WKEY_SPLIT, :])
+        nc.scalar.copy(out=wkey_bf[:, WKEY_SPLIT:, :], in_=wkey_stepped[:, WKEY_SPLIT:, :])
+        wkey_mx = quantize("wkey", wkey_bf[:].rearrange("p m j -> p (m j)"), M)
+        a_ps = ps.tile([P, M], F32, name="a_ps", tag="win")
+        product(a_ps[:], query_mx, wkey_mx, slice(0, M), True, True)
+        got_words = tile("got_words", [P, I], U32)
+        nc.vector.tensor_copy(out=got_words[:], in_=key_words[:].indirect(offsets[:]))
+        b_ps = ps.tile([P, I], F32, name="b_ps", tag="mem")
+        product(b_ps[:], query_mx, (got_words, got_bytes), slice(0, I), True, True)
+
+        sums = tile("sums", [P, 2], F32)
+
+        def exps(name, scores, neg_max, total):
+            dealt = tile(name + "_exp", [P, PACK, P], F32)
+            nc.scalar.activation(
+                out=dealt[:],
+                in_=scores[:].rearrange("q (s r) -> q r s", r=PACK),
+                func=ACT.Exp,
+                bias=neg_max[:],
+                scale=1.0,
+                accum_out=total,
+            )
+            return dealt
+
+        neg_amax = tile("neg_amax", [P, 1], F32)
+        nc.vector.tensor_reduce(out=neg_amax[:], in_=a_ps[:], axis=AX.X, op=ALU.max, negate=True)
+        p_exp = exps("p", a_ps, neg_amax, sums[:, 1:2])
+        neg_z = tile("neg_z", [P, 1], F32)
+        nc.vector.tensor_reduce(out=neg_z[:], in_=b_ps[:], axis=AX.X, op=ALU.max, negate=True)
+        r_exp = exps("r", b_ps, neg_z, sums[:, 0:1])
+
+        signs = tile("signs", [P, 2], F32)
+        nc.gpsimd.memset(signs[:, 0:1], -1.0)
+        nc.gpsimd.memset(signs[:, 1:2], 1.0)
+        neg_x = tile("neg_x", [P, 1], F32)
+        nc.vector.tensor_scalar(neg_x[:], neg_z[:], th_col[:], steep_col[:], ALU.add, ALU.mult)
+        gate_arg = tile("gate_arg", [P, 2], F32)
+        nc.vector.tensor_scalar(gate_arg[:], signs[:], neg_x[:], 0.0, ALU.mult, ALU.min)
+        gate_exp = tile("gate_exp", [P, 2], F32)
+        gate_sum = tile("gate_sum", [P, 1], F32)
+        nc.scalar.activation(out=gate_exp[:], in_=gate_arg[:], func=ACT.Exp, accum_out=gate_sum[:])
+        denom = tile("denom", [P, 2], F32)
+        nc.vector.tensor_scalar(denom[:], sums[:], gate_sum[:], None, ALU.mult)
+        recip = tile("recip", [P, 2], F32)
+        nc.vector.reciprocal(recip[:], denom[:])
+
+        def weights(name, dealt, col, factor4, tag):
+            scaled = tile(name + "_scaled", [P, PACK, P], F32)
+            nc.vector.tensor_scalar(
+                scaled[:], dealt[:], recip[:, col : col + 1], gate_exp[:, col : col + 1], ALU.mult, ALU.mult
+            )
+            turned = ps.tile([P, PACK, Q], F32, name=name + "_turned", tag=tag)
+            for r in range(PACK):
+                nc.tensor.transpose(turned[:, r, :], scaled[:, r, :], ident[:])
+            grouped = tile(name + "_bf", [P, Q, PACK], BF16)
+            nc.vector.tensor_tensor(
+                grouped[:],
+                turned[:].rearrange("s r q -> s q r"),
+                factor4[:].unsqueeze(1).to_broadcast([P, Q, PACK]),
+                ALU.mult,
+            )
+            return quantize(name, grouped[:].rearrange("s q r -> s (q r)"), Q)
+
+        def gather_values(j):
+            got = tile("got_vals%d" % j, [P, I], BF16, "gate_arg" if j == 0 else None)
+            if j == BLOCKS - 1:
+                half, cols = GATHER_SPLIT, GATHER_SPLIT // 16
+                nc.vector.tensor_copy(out=got[:, :half], in_=vals_raw[j][:].indirect(offsets[:, :cols]))
+                nc.scalar.activation(out=got[:, half:], in_=vals_raw[j][:].indirect(offsets[:, cols:]), func=ACT.Copy)
+            else:
+                nc.scalar.activation(out=got[:], in_=vals_raw[j][:].indirect(offsets[:]), func=ACT.Copy)
+            return got
+
+        def values(name, gots, turned, tag):
+            count = len(gots)
+            for c, got in enumerate(gots):
+                pairs = got[:].bitcast(F32)
+                for u in range(2):
+                    nc.tensor.transpose(turned[:, c, u, :], pairs[:, u : I // 2 : 2], ident[:])
+            grouped = tile(name + "_bf", [P, count * P * PACK], BF16, tag)
+            nc.scalar.copy(
+                out=grouped[:].bitcast(F32).rearrange("s (c e u) -> s c e u", c=count, u=2),
+                in_=turned[:].rearrange("s c u e -> s c e u"),
+            )
+            return quantize(name, grouped[:], count * P)
+
+        wt_mx = weights("wt", p_exp, 1, wf4, "win")
+        ut_mx = weights("ut", r_exp, 0, size4, "mem")
+        acc = [ps.tile([P, P], F32, name="acc%d" % j) for j in range(BLOCKS)]
+        gots = [gather_values(j) for j in range(3)]
+        vt_mx = values("vt01", gots[:2], ps.tile([P, 2, 2, P], F32, name="turned01", tag="win"), "vals_raw2")
+        for j in range(2):
+            product(acc[j][:], ut_mx, vt_mx, slice(j * P, (j + 1) * P), True, False)
+        for j in range(2, BLOCKS):
+            got = gots[j] if j == 2 else gather_values(j)
+            vt_mx = values("vt%d" % j, [got], ps.tile([P, 1, 2, P], F32, name="turned%d" % j), None)
+            product(acc[j][:], ut_mx, vt_mx, slice(0, P), True, False)
+
+        for n, blocks in enumerate(WVAL_LOADS):
+            width = P * len(blocks)
+            grouped = tile("wval_bf%d" % n, [P, width, PACK], BF16)
+            stepped = wval_raw[n][:].rearrange("p j e -> p e j")
+            if n == 1:
+                nc.scalar.copy(out=grouped[:], in_=stepped)
+            else:
+                nc.vector.tensor_copy(out=grouped[:], in_=stepped)
+            wval_mx = quantize("wval%d" % n, grouped[:].rearrange("p e j -> p (e j)"), width)
+            for c, j in enumerate(blocks):
+                product(acc[j][:], wt_mx, wval_mx, slice(c * P, (c + 1) * P), False, True)
+                result = tile("result%d" % j, [P, P], F32)
+                nc.scalar.copy(out=result[:], in_=acc[j][:])
+                nc.sync.dma_start(out=out[:, j * P : (j + 1) * P], in_=result[:])

@@ -20,8 +20,8 @@ AX = mybir.AxisListType
 P = 128
 PACK = 4
 BLOCKS = E // P
-WKEY_SPLIT = 256
-GATHER_SPLIT = 288
+WKEY_VECTOR = 96
+GATHER_SPLIT = 320
 WVAL_LOADS = ((2, 3), (1,), (0,))
 
 
@@ -36,11 +36,16 @@ def tile_attend_confidencegate_kernel(
         def tile(name, shape, dtype, tag=None):
             return sb.tile(shape, dtype, name=name, tag=tag or name, align_bytes=64)
 
+        def mx_tiles(name, width, tag=None):
+            return tile(name + "_codes", [P, width], U32, tag), tile(name + "_scales", [P, width], U8)
+
+        def quantize_into(mx, cols, grouped):
+            nc.vector.quantize_mx(out=mx[0][:, cols].bitcast(FP8X4), scales=mx[1][:, cols], in_=grouped)
+
         def quantize(name, grouped, width):
-            codes = tile(name + "_codes", [P, width], U32)
-            scales = tile(name + "_scales", [P, width], U8)
-            nc.vector.quantize_mx(out=codes[:].bitcast(FP8X4), scales=scales[:], in_=grouped)
-            return codes, scales
+            mx = mx_tiles(name, width)
+            quantize_into(mx, slice(0, width), grouped)
+            return mx
 
         def product(acc, lhs, rhs, cols, start, stop):
             nc.tensor.matmul_mx(
@@ -55,32 +60,34 @@ def tile_attend_confidencegate_kernel(
 
         query_raw = tile("query_raw", [P, PACK, Q], F32)
         nc.sync.dma_start(out=query_raw[:], in_=query.rearrange("(p j) q -> p j q", j=PACK))
-        scale_rows = tile("scale_rows", [P, T // 4], I32)
-        for quad in range(4):
-            nc.sync.dma_start(
-                out=scale_rows[32 * quad : 32 * quad + 4, :],
-                in_=keys_scales[0, 4 * quad : 4 * quad + 4, :].bitcast(I32),
-            )
         offsets = sb.tile([P, I // 16], U16, name="offsets")
         nc.sync.dma_start(offsets[:], offs)
-        wkey_raw = tile("wkey_raw", [P, PACK, M], F32)
-        nc.sync.dma_start(out=wkey_raw[:], in_=wkey.rearrange("(p j) m -> p j m", j=PACK))
+        key_bytes = tile("key_bytes", [P, T], U8)
+        nc.vector.memset(key_bytes[:].bitcast(I32), 0)
+        for quad in range(4):
+            nc.sync.dma_start(
+                out=key_bytes[32 * quad : 32 * quad + 4, :].bitcast(I32),
+                in_=keys_scales[0, 4 * quad : 4 * quad + 4, :].bitcast(I32),
+            )
         key_words = tile("key_words", [P, T], U32)
         nc.sync.dma_start(
             out=key_words[:].bitcast(I32),
             in_=keys_words[0].rearrange("p n t -> p (n t)").bitcast(I32),
         )
+        wkey_rows = wkey.rearrange("(p j) m -> p j m", j=PACK)
+        wkey_raw = [tile("wkey_raw%d" % h, [P, PACK, M // 2], F32) for h in range(2)]
+        for h in range(2):
+            nc.sync.dma_start(out=wkey_raw[h][:], in_=wkey_rows[:, :, h * M // 2 : (h + 1) * M // 2])
         th_col = tile("th_col", [P, 1], F32)
         nc.sync.dma_start(out=th_col[:], in_=th)
         steep_col = tile("steep_col", [P, 1], F32)
         nc.sync.dma_start(out=steep_col[:], in_=steep)
         vals_raw = [tile("vals_raw%d" % j, [P, T], F32) for j in range(BLOCKS)]
-        nc.sync.dma_start(out=vals_raw[0][:], in_=vals[:P, :])
         size4 = tile("size4", [P, PACK], F32)
         nc.sync.dma_start(out=size4[:], in_=size.rearrange("o (p r) -> (o p) r", r=PACK))
         wf4 = tile("wf4", [P, PACK], F32)
         nc.sync.dma_start(out=wf4[:], in_=wf.rearrange("o (p r) -> (o p) r", r=PACK))
-        for j in range(1, BLOCKS):
+        for j in range(BLOCKS):
             nc.sync.dma_start(out=vals_raw[j][:], in_=vals[j * P : (j + 1) * P, :])
         wval_rows = wval.rearrange("(p j) e -> p j e", j=PACK)
         wval_raw = []
@@ -94,46 +101,50 @@ def tile_attend_confidencegate_kernel(
 
         query_bf = tile("query_bf", [P, Q, PACK], BF16)
         nc.scalar.activation(out=query_bf[:], in_=query_raw[:].rearrange("p j q -> p q j"), func=ACT.Copy)
-        key_bytes = tile("key_bytes", [P, T], U8)
-        nc.vector.memset(key_bytes[:].bitcast(I32), 0)
-        for quad in range(4):
-            rows = slice(32 * quad, 32 * quad + 4)
-            nc.vector.tensor_copy(out=key_bytes[rows, :].bitcast(I32), in_=scale_rows[rows, :])
-        query_mx = quantize("query", query_bf[:].rearrange("p q j -> p (q j)"), Q)
         got_bytes = tile("got_bytes", [P, I], U8)
         nc.vector.tensor_copy(out=got_bytes[:], in_=key_bytes[:].indirect(offsets[:]))
-        wkey_bf = tile("wkey_bf", [P, M, PACK], BF16)
-        wkey_stepped = wkey_raw[:].rearrange("p j m -> p m j")
-        nc.vector.tensor_copy(out=wkey_bf[:, :WKEY_SPLIT, :], in_=wkey_stepped[:, :WKEY_SPLIT, :])
-        nc.scalar.copy(out=wkey_bf[:, WKEY_SPLIT:, :], in_=wkey_stepped[:, WKEY_SPLIT:, :])
-        wkey_mx = quantize("wkey", wkey_bf[:].rearrange("p m j -> p (m j)"), M)
-        a_ps = ps.tile([P, M], F32, name="a_ps", tag="win")
-        product(a_ps[:], query_mx, wkey_mx, slice(0, M), True, True)
+        query_mx = quantize("query", query_bf[:].rearrange("p q j -> p (q j)"), Q)
         got_words = tile("got_words", [P, I], U32)
         nc.vector.tensor_copy(out=got_words[:], in_=key_words[:].indirect(offsets[:]))
         b_ps = ps.tile([P, I], F32, name="b_ps", tag="mem")
         product(b_ps[:], query_mx, (got_words, got_bytes), slice(0, I), True, True)
+        neg_z = tile("neg_z", [P, 1], F32)
+        nc.vector.tensor_reduce(out=neg_z[:], in_=b_ps[:], axis=AX.X, op=ALU.max, negate=True)
 
-        sums = tile("sums", [P, 2], F32)
+        wkey_bf = tile("wkey_bf", [P, M, PACK], BF16)
+        first, second = (raw[:].rearrange("p j m -> p m j") for raw in wkey_raw)
+        split = M // 2 - WKEY_VECTOR
+        nc.scalar.copy(out=wkey_bf[:, : M // 2, :], in_=first)
+        nc.scalar.copy(out=wkey_bf[:, M // 2 : M - WKEY_VECTOR, :], in_=second[:, :split, :])
+        nc.vector.tensor_copy(out=wkey_bf[:, M - WKEY_VECTOR :, :], in_=second[:, split:, :])
+        wkey_mx = quantize("wkey", wkey_bf[:].rearrange("p m j -> p (m j)"), M)
+        a_ps = ps.tile([P, M], F32, name="a_ps", tag="win")
+        product(a_ps[:], query_mx, wkey_mx, slice(0, M), True, True)
 
-        def exps(name, scores, neg_max, total):
-            dealt = tile(name + "_exp", [P, PACK, P], F32)
+        def gather_values(j):
+            got = tile("got_vals%d" % j, [P, I], BF16)
+            if j == BLOCKS - 1:
+                half, cols = GATHER_SPLIT, GATHER_SPLIT // 16
+                nc.vector.tensor_copy(out=got[:, :half], in_=vals_raw[j][:].indirect(offsets[:, :cols]))
+                nc.scalar.activation(out=got[:, half:], in_=vals_raw[j][:].indirect(offsets[:, cols:]), func=ACT.Copy)
+            else:
+                nc.scalar.activation(out=got[:], in_=vals_raw[j][:].indirect(offsets[:]), func=ACT.Copy)
+            return got
+
+        def exps(name, scores, neg_max, tag):
+            dealt = tile(name + "_exp", [P, PACK, P], F32, tag)
+            total = tile(name + "_sum", [P, 1], F32)
             nc.scalar.activation(
                 out=dealt[:],
                 in_=scores[:].rearrange("q (s r) -> q r s", r=PACK),
                 func=ACT.Exp,
                 bias=neg_max[:],
                 scale=1.0,
-                accum_out=total,
+                accum_out=total[:],
             )
-            return dealt
+            return dealt, total
 
-        neg_amax = tile("neg_amax", [P, 1], F32)
-        nc.vector.tensor_reduce(out=neg_amax[:], in_=a_ps[:], axis=AX.X, op=ALU.max, negate=True)
-        p_exp = exps("p", a_ps, neg_amax, sums[:, 1:2])
-        neg_z = tile("neg_z", [P, 1], F32)
-        nc.vector.tensor_reduce(out=neg_z[:], in_=b_ps[:], axis=AX.X, op=ALU.max, negate=True)
-        r_exp = exps("r", b_ps, neg_z, sums[:, 0:1])
+        r_exp, r_sum = exps("r", b_ps, neg_z, "wkey_raw1")
 
         signs = tile("signs", [P, 2], F32)
         nc.gpsimd.memset(signs[:, 0:1], -1.0)
@@ -145,16 +156,18 @@ def tile_attend_confidencegate_kernel(
         gate_exp = tile("gate_exp", [P, 2], F32)
         gate_sum = tile("gate_sum", [P, 1], F32)
         nc.scalar.activation(out=gate_exp[:], in_=gate_arg[:], func=ACT.Exp, accum_out=gate_sum[:])
-        denom = tile("denom", [P, 2], F32)
-        nc.vector.tensor_scalar(denom[:], sums[:], gate_sum[:], None, ALU.mult)
-        recip = tile("recip", [P, 2], F32)
-        nc.vector.reciprocal(recip[:], denom[:])
 
-        def weights(name, dealt, col, factor4, tag):
+        neg_amax = tile("neg_amax", [P, 1], F32)
+        nc.vector.tensor_reduce(out=neg_amax[:], in_=a_ps[:], axis=AX.X, op=ALU.max, negate=True)
+        p_exp, p_sum = exps("p", a_ps, neg_amax, None)
+
+        def weights(name, dealt, total, col, factor4, tag):
+            denom = tile(name + "_denom", [P, 1], F32)
+            nc.vector.tensor_tensor(denom[:], total[:], gate_sum[:], ALU.mult)
+            recip = tile(name + "_recip", [P, 1], F32)
+            nc.vector.reciprocal(recip[:], denom[:])
             scaled = tile(name + "_scaled", [P, PACK, P], F32)
-            nc.vector.tensor_scalar(
-                scaled[:], dealt[:], recip[:, col : col + 1], gate_exp[:, col : col + 1], ALU.mult, ALU.mult
-            )
+            nc.vector.tensor_scalar(scaled[:], dealt[:], recip[:], gate_exp[:, col : col + 1], ALU.mult, ALU.mult)
             turned = ps.tile([P, PACK, Q], F32, name=name + "_turned", tag=tag)
             for r in range(PACK):
                 nc.tensor.transpose(turned[:, r, :], scaled[:, r, :], ident[:])
@@ -167,40 +180,32 @@ def tile_attend_confidencegate_kernel(
             )
             return quantize(name, grouped[:].rearrange("s q r -> s (q r)"), Q)
 
-        def gather_values(j):
-            got = tile("got_vals%d" % j, [P, I], BF16, "gate_arg" if j == 0 else None)
-            if j == BLOCKS - 1:
-                half, cols = GATHER_SPLIT, GATHER_SPLIT // 16
-                nc.vector.tensor_copy(out=got[:, :half], in_=vals_raw[j][:].indirect(offsets[:, :cols]))
-                nc.scalar.activation(out=got[:, half:], in_=vals_raw[j][:].indirect(offsets[:, cols:]), func=ACT.Copy)
-            else:
-                nc.scalar.activation(out=got[:], in_=vals_raw[j][:].indirect(offsets[:]), func=ACT.Copy)
-            return got
-
-        def values(name, gots, turned, tag):
-            count = len(gots)
-            for c, got in enumerate(gots):
-                pairs = got[:].bitcast(F32)
+        def values(name, blocks, bank_tag, copy):
+            count = len(blocks)
+            turned = ps.tile([P, count, 2, P], F32, name=name + "_turned", tag=bank_tag)
+            for c, j in enumerate(blocks):
+                pairs = gots[j][:].bitcast(F32)
                 for u in range(2):
                     nc.tensor.transpose(turned[:, c, u, :], pairs[:, u : I // 2 : 2], ident[:])
-            grouped = tile(name + "_bf", [P, count * P * PACK], BF16, tag)
-            nc.scalar.copy(
+            grouped = tile(name + "_bf", [P, count * P * PACK], BF16)
+            copy(
                 out=grouped[:].bitcast(F32).rearrange("s (c e u) -> s c e u", c=count, u=2),
                 in_=turned[:].rearrange("s c u e -> s c e u"),
             )
-            return quantize(name, grouped[:], count * P)
+            return grouped[:]
 
-        wt_mx = weights("wt", p_exp, 1, wf4, "win")
-        ut_mx = weights("ut", r_exp, 0, size4, "mem")
-        acc = [ps.tile([P, P], F32, name="acc%d" % j) for j in range(BLOCKS)]
-        gots = [gather_values(j) for j in range(3)]
-        vt_mx = values("vt01", gots[:2], ps.tile([P, 2, 2, P], F32, name="turned01", tag="win"), "vals_raw2")
-        for j in range(2):
-            product(acc[j][:], ut_mx, vt_mx, slice(j * P, (j + 1) * P), True, False)
-        for j in range(2, BLOCKS):
-            got = gots[j] if j == 2 else gather_values(j)
-            vt_mx = values("vt%d" % j, [got], ps.tile([P, 1, 2, P], F32, name="turned%d" % j), None)
-            product(acc[j][:], ut_mx, vt_mx, slice(0, P), True, False)
+        ut_mx = weights("ut", r_exp, r_sum, 0, size4, "mem")
+        wt_mx = weights("wt", p_exp, p_sum, 1, wf4, "win")
+        gots = [gather_values(j) for j in range(BLOCKS)]
+        acc = [ps.tile([P, P * len(blocks)], F32, name="acc%d" % n) for n, blocks in enumerate(WVAL_LOADS)]
+        early_mx = mx_tiles("vt_early", 3 * P, "vals_raw3")
+        quantize_into(early_mx, slice(0, 2 * P), values("vt01", (0, 1), "pair", nc.vector.tensor_copy))
+        quantize_into(early_mx, slice(2 * P, 3 * P), values("vt2", (2,), "win", nc.scalar.copy))
+        last_mx = quantize("vt_last", values("vt3", (3,), "mem", nc.scalar.copy), P)
+        product(acc[2][:], ut_mx, early_mx, slice(0, P), True, False)
+        product(acc[1][:], ut_mx, early_mx, slice(P, 2 * P), True, False)
+        product(acc[0][:, :P], ut_mx, early_mx, slice(2 * P, 3 * P), True, False)
+        product(acc[0][:, P:], ut_mx, last_mx, slice(0, P), False, False)
 
         for n, blocks in enumerate(WVAL_LOADS):
             width = P * len(blocks)
@@ -211,8 +216,7 @@ def tile_attend_confidencegate_kernel(
             else:
                 nc.vector.tensor_copy(out=grouped[:], in_=stepped)
             wval_mx = quantize("wval%d" % n, grouped[:].rearrange("p e j -> p (e j)"), width)
-            for c, j in enumerate(blocks):
-                product(acc[j][:], wt_mx, wval_mx, slice(c * P, (c + 1) * P), False, True)
-                result = tile("result%d" % j, [P, P], F32)
-                nc.scalar.copy(out=result[:], in_=acc[j][:])
-                nc.sync.dma_start(out=out[:, j * P : (j + 1) * P], in_=result[:])
+            product(acc[n][:], wt_mx, wval_mx, slice(0, width), False, True)
+            result = tile("result%d" % n, [P, width], F32)
+            nc.scalar.copy(out=result[:], in_=acc[n][:])
+            nc.sync.dma_start(out=out[:, blocks[0] * P : (blocks[-1] + 1) * P], in_=result[:])

@@ -58,6 +58,15 @@ def tile_attend_confidencegate_kernel(
                 stop=stop,
             )
 
+        def interleave(copy, grouped, raw, cols):
+            copy(
+                out=grouped[:, cols[0], :].rearrange("p (c i) j -> p c j i", i=PACK),
+                in_=raw[:, :, cols[1]].rearrange("p j (c i) -> p c j i", i=PACK),
+            )
+
+        def activation_copy(out, in_):
+            nc.scalar.activation(out=out, in_=in_, func=ACT.Copy)
+
         query_raw = tile("query_raw", [P, PACK, Q], F32)
         nc.sync.dma_start(out=query_raw[:], in_=query.rearrange("(p j) q -> p j q", j=PACK))
         offsets = sb.tile([P, I // 16], U16, name="offsets")
@@ -100,7 +109,7 @@ def tile_attend_confidencegate_kernel(
         make_identity(nc, ident[:])
 
         query_bf = tile("query_bf", [P, Q, PACK], BF16)
-        nc.scalar.activation(out=query_bf[:], in_=query_raw[:].rearrange("p j q -> p q j"), func=ACT.Copy)
+        interleave(activation_copy, query_bf, query_raw, (slice(0, Q), slice(0, Q)))
         got_bytes = tile("got_bytes", [P, I], U8)
         nc.vector.tensor_copy(out=got_bytes[:], in_=key_bytes[:].indirect(offsets[:]))
         query_mx = quantize("query", query_bf[:].rearrange("p q j -> p (q j)"), Q)
@@ -112,11 +121,11 @@ def tile_attend_confidencegate_kernel(
         nc.vector.tensor_reduce(out=neg_z[:], in_=b_ps[:], axis=AX.X, op=ALU.max, negate=True)
 
         wkey_bf = tile("wkey_bf", [P, M, PACK], BF16)
-        first, second = (raw[:].rearrange("p j m -> p m j") for raw in wkey_raw)
-        split = M // 2 - WKEY_VECTOR
-        nc.scalar.copy(out=wkey_bf[:, : M // 2, :], in_=first)
-        nc.scalar.copy(out=wkey_bf[:, M // 2 : M - WKEY_VECTOR, :], in_=second[:, :split, :])
-        nc.vector.tensor_copy(out=wkey_bf[:, M - WKEY_VECTOR :, :], in_=second[:, split:, :])
+        half = M // 2
+        split = half - WKEY_VECTOR
+        interleave(nc.scalar.copy, wkey_bf, wkey_raw[0], (slice(0, half), slice(0, half)))
+        interleave(nc.scalar.copy, wkey_bf, wkey_raw[1], (slice(half, half + split), slice(0, split)))
+        interleave(nc.vector.tensor_copy, wkey_bf, wkey_raw[1], (slice(half + split, M), slice(split, half)))
         wkey_mx = quantize("wkey", wkey_bf[:].rearrange("p m j -> p (m j)"), M)
         a_ps = ps.tile([P, M], F32, name="a_ps", tag="win")
         product(a_ps[:], query_mx, wkey_mx, slice(0, M), True, True)
@@ -124,9 +133,9 @@ def tile_attend_confidencegate_kernel(
         def gather_values(j):
             got = tile("got_vals%d" % j, [P, I], BF16)
             if j == BLOCKS - 1:
-                half, cols = GATHER_SPLIT, GATHER_SPLIT // 16
-                nc.vector.tensor_copy(out=got[:, :half], in_=vals_raw[j][:].indirect(offsets[:, :cols]))
-                nc.scalar.activation(out=got[:, half:], in_=vals_raw[j][:].indirect(offsets[:, cols:]), func=ACT.Copy)
+                cut, cols = GATHER_SPLIT, GATHER_SPLIT // 16
+                nc.vector.tensor_copy(out=got[:, :cut], in_=vals_raw[j][:].indirect(offsets[:, :cols]))
+                nc.scalar.activation(out=got[:, cut:], in_=vals_raw[j][:].indirect(offsets[:, cols:]), func=ACT.Copy)
             else:
                 nc.scalar.activation(out=got[:], in_=vals_raw[j][:].indirect(offsets[:]), func=ACT.Copy)
             return got
@@ -210,11 +219,14 @@ def tile_attend_confidencegate_kernel(
         for n, blocks in enumerate(WVAL_LOADS):
             width = P * len(blocks)
             grouped = tile("wval_bf%d" % n, [P, width, PACK], BF16)
-            stepped = wval_raw[n][:].rearrange("p j e -> p e j")
-            if n == 1:
-                nc.scalar.copy(out=grouped[:], in_=stepped)
+            whole, low, high = slice(0, width), slice(0, width // 2), slice(width // 2, width)
+            if n == 0:
+                interleave(nc.vector.tensor_copy, grouped, wval_raw[n], (whole, whole))
+            elif n == 1:
+                interleave(nc.scalar.copy, grouped, wval_raw[n], (whole, whole))
             else:
-                nc.vector.tensor_copy(out=grouped[:], in_=stepped)
+                interleave(nc.vector.tensor_copy, grouped, wval_raw[n], (low, low))
+                interleave(nc.scalar.copy, grouped, wval_raw[n], (high, high))
             wval_mx = quantize("wval%d" % n, grouped[:].rearrange("p e j -> p (e j)"), width)
             product(acc[n][:], wt_mx, wval_mx, slice(0, width), False, True)
             result = tile("result%d" % n, [P, width], F32)

from contextlib import ExitStack

import concourse.mybir as mybir
from concourse.masks import make_identity

D, T, I, Q, E, M = 512, 2048, 512, 128, 512, 512
FLOPS = 2 * Q * (D * M + D * I + M * E + I * E)

F32 = mybir.dt.float32
BF16 = mybir.dt.bfloat16
I32 = mybir.dt.int32
U32 = mybir.dt.uint32
U16 = mybir.dt.uint16
U8 = mybir.dt.uint8
FP8X4 = mybir.dt.float8_e4m3fn_x4
ALU = mybir.AluOpType
ACT = mybir.ActivationFunctionType
AX = mybir.AxisListType

P = 128
PACK = 4
BLOCKS = E // P
WKEY_VECTOR = 96
GATHER_SPLIT = 320
WVAL_LOADS = ((2, 3), (1,), (0,))


def tile_attend_confidencegate_kernel(
    tc, query, wkey, wval, keys_words, keys_scales, vals, th, steep, wf, size, offs, out
):
    nc = tc.nc
    with ExitStack() as ctx:
        sb = ctx.enter_context(tc.tile_pool(name="sb", bufs=1))
        ps = ctx.enter_context(tc.psum_pool(name="ps", bufs=1))

        def tile(name, shape, dtype, tag=None):
            return sb.tile(shape, dtype, name=name, tag=tag or name, align_bytes=64)

        def mx_tiles(name, width, tag=None):
            return tile(name + "_codes", [P, width], U32, tag), tile(name + "_scales", [P, width], U8)

        def quantize_into(mx, cols, grouped):
            nc.vector.quantize_mx(out=mx[0][:, cols].bitcast(FP8X4), scales=mx[1][:, cols], in_=grouped)

        def quantize(name, grouped, width):
            mx = mx_tiles(name, width)
            quantize_into(mx, slice(0, width), grouped)
            return mx

        def product(acc, lhs, rhs, cols, start, stop):
            nc.tensor.matmul_mx(
                out=acc,
                lhsT=lhs[0][:].bitcast(FP8X4),
                lhsT_scale=lhs[1][:],
                rhs=rhs[0][:, cols].bitcast(FP8X4),
                rhs_scale=rhs[1][:, cols],
                start=start,
                stop=stop,
            )

        def interleave(copy, grouped, raw, cols):
            copy(
                out=grouped[:, cols[0], :].rearrange("p (c i) j -> p c j i", i=PACK),
                in_=raw[:, :, cols[1]].rearrange("p j (c i) -> p c j i", i=PACK),
            )

        def activation_copy(out, in_):
            nc.scalar.activation(out=out, in_=in_, func=ACT.Copy)

        query_raw = tile("query_raw", [P, PACK, Q], F32)
        nc.sync.dma_start(out=query_raw[:], in_=query.rearrange("(p j) q -> p j q", j=PACK))
        offsets = sb.tile([P, I // 16], U16, name="offsets")
        nc.sync.dma_start(offsets[:], offs)
        key_bytes = tile("key_bytes", [P, T], U8)
        nc.vector.memset(key_bytes[:].bitcast(I32), 0)
        for quad in range(4):
            nc.sync.dma_start(
                out=key_bytes[32 * quad : 32 * quad + 4, :].bitcast(I32),
                in_=keys_scales[0, 4 * quad : 4 * quad + 4, :].bitcast(I32),
            )
        key_words = tile("key_words", [P, T], U32)
        nc.sync.dma_start(
            out=key_words[:].bitcast(I32),
            in_=keys_words[0].rearrange("p n t -> p (n t)").bitcast(I32),
        )
        wkey_rows = wkey.rearrange("(p j) m -> p j m", j=PACK)
        wkey_raw = [tile("wkey_raw%d" % h, [P, PACK, M // 2], F32) for h in range(2)]
        for h in range(2):
            nc.sync.dma_start(out=wkey_raw[h][:], in_=wkey_rows[:, :, h * M // 2 : (h + 1) * M // 2])
        th_col = tile("th_col", [P, 1], F32)
        nc.sync.dma_start(out=th_col[:], in_=th)
        steep_col = tile("steep_col", [P, 1], F32)
        nc.sync.dma_start(out=steep_col[:], in_=steep)
        vals_raw = [tile("vals_raw%d" % j, [P, T], F32) for j in range(BLOCKS)]
        size4 = tile("size4", [P, PACK], F32)
        nc.sync.dma_start(out=size4[:], in_=size.rearrange("o (p r) -> (o p) r", r=PACK))
        wf4 = tile("wf4", [P, PACK], F32)
        nc.sync.dma_start(out=wf4[:], in_=wf.rearrange("o (p r) -> (o p) r", r=PACK))
        for j in range(BLOCKS):
            nc.sync.dma_start(out=vals_raw[j][:], in_=vals[j * P : (j + 1) * P, :])
        wval_rows = wval.rearrange("(p j) e -> p j e", j=PACK)
        wval_raw = []
        for n, blocks in enumerate(WVAL_LOADS):
            raw = tile("wval_raw%d" % n, [P, PACK, P * len(blocks)], F32)
            nc.sync.dma_start(out=raw[:], in_=wval_rows[:, :, blocks[0] * P : (blocks[-1] + 1) * P])
            wval_raw.append(raw)

        ident = tile("ident", [P, P], F32)
        make_identity(nc, ident[:])

        query_bf = tile("query_bf", [P, Q, PACK], BF16)
        interleave(activation_copy, query_bf, query_raw, (slice(0, Q), slice(0, Q)))
        got_bytes = tile("got_bytes", [P, I], U8)
        nc.vector.tensor_copy(out=got_bytes[:], in_=key_bytes[:].indirect(offsets[:]))
        query_mx = quantize("query", query_bf[:].rearrange("p q j -> p (q j)"), Q)
        got_words = tile("got_words", [P, I], U32)
        nc.vector.tensor_copy(out=got_words[:], in_=key_words[:].indirect(offsets[:]))
        b_ps = ps.tile([P, I], F32, name="b_ps", tag="mem")
        product(b_ps[:], query_mx, (got_words, got_bytes), slice(0, I), True, True)
        neg_z = tile("neg_z", [P, 1], F32)
        nc.vector.tensor_reduce(out=neg_z[:], in_=b_ps[:], axis=AX.X, op=ALU.max, negate=True)

        wkey_bf = tile("wkey_bf", [P, M, PACK], BF16)
        half = M // 2
        split = half - WKEY_VECTOR
        interleave(nc.scalar.copy, wkey_bf, wkey_raw[0], (slice(0, half), slice(0, half)))
        interleave(nc.scalar.copy, wkey_bf, wkey_raw[1], (slice(half, half + split), slice(0, split)))
        interleave(nc.vector.tensor_copy, wkey_bf, wkey_raw[1], (slice(half + split, M), slice(split, half)))
        wkey_mx = quantize("wkey", wkey_bf[:].rearrange("p m j -> p (m j)"), M)
        a_ps = ps.tile([P, M], F32, name="a_ps", tag="win")
        product(a_ps[:], query_mx, wkey_mx, slice(0, M), True, True)

        def gather_values(j):
            got = tile("got_vals%d" % j, [P, I], BF16)
            if j == BLOCKS - 1:
                cut, cols = GATHER_SPLIT, GATHER_SPLIT // 16
                nc.vector.tensor_copy(out=got[:, :cut], in_=vals_raw[j][:].indirect(offsets[:, :cols]))
                nc.scalar.activation(out=got[:, cut:], in_=vals_raw[j][:].indirect(offsets[:, cols:]), func=ACT.Copy)
            else:
                nc.scalar.activation(out=got[:], in_=vals_raw[j][:].indirect(offsets[:]), func=ACT.Copy)
            return got

        def exps(name, scores, neg_max, tag):
            dealt = tile(name + "_exp", [P, PACK, P], F32, tag)
            total = tile(name + "_sum", [P, 1], F32)
            nc.scalar.activation(
                out=dealt[:],
                in_=scores[:].rearrange("q (s r) -> q r s", r=PACK),
                func=ACT.Exp,
                bias=neg_max[:],
                scale=1.0,
                accum_out=total[:],
            )
            return dealt, total

        r_exp, r_sum = exps("r", b_ps, neg_z, "wkey_raw1")

        signs = tile("signs", [P, 2], F32)
        nc.gpsimd.memset(signs[:, 0:1], -1.0)
        nc.gpsimd.memset(signs[:, 1:2], 1.0)
        neg_x = tile("neg_x", [P, 1], F32)
        nc.vector.tensor_scalar(neg_x[:], neg_z[:], th_col[:], steep_col[:], ALU.add, ALU.mult)
        gate_arg = tile("gate_arg", [P, 2], F32)
        nc.vector.tensor_scalar(gate_arg[:], signs[:], neg_x[:], 0.0, ALU.mult, ALU.min)
        gate_exp = tile("gate_exp", [P, 2], F32)
        gate_sum = tile("gate_sum", [P, 1], F32)
        nc.scalar.activation(out=gate_exp[:], in_=gate_arg[:], func=ACT.Exp, accum_out=gate_sum[:])

        neg_amax = tile("neg_amax", [P, 1], F32)
        nc.vector.tensor_reduce(out=neg_amax[:], in_=a_ps[:], axis=AX.X, op=ALU.max, negate=True)
        p_exp, p_sum = exps("p", a_ps, neg_amax, None)

        def weights(name, dealt, total, col, factor4, tag):
            denom = tile(name + "_denom", [P, 1], F32)
            nc.vector.tensor_tensor(denom[:], total[:], gate_sum[:], ALU.mult)
            recip = tile(name + "_recip", [P, 1], F32)
            nc.vector.reciprocal(recip[:], denom[:])
            scaled = tile(name + "_scaled", [P, PACK, P], F32)
            nc.vector.tensor_scalar(scaled[:], dealt[:], recip[:], gate_exp[:, col : col + 1], ALU.mult, ALU.mult)
            turned = ps.tile([P, PACK, Q], F32, name=name + "_turned", tag=tag)
            for r in range(PACK):
                nc.tensor.transpose(turned[:, r, :], scaled[:, r, :], ident[:])
            grouped = tile(name + "_bf", [P, Q, PACK], BF16)
            nc.vector.tensor_tensor(
                grouped[:],
                turned[:].rearrange("s r q -> s q r"),
                factor4[:].unsqueeze(1).to_broadcast([P, Q, PACK]),
                ALU.mult,
            )
            return quantize(name, grouped[:].rearrange("s q r -> s (q r)"), Q)

        def values(name, blocks, bank_tag, copy):
            count = len(blocks)
            turned = ps.tile([P, count, 2, P], F32, name=name + "_turned", tag=bank_tag)
            for c, j in enumerate(blocks):
                pairs = gots[j][:].bitcast(F32)
                for u in range(2):
                    nc.tensor.transpose(turned[:, c, u, :], pairs[:, u : I // 2 : 2], ident[:])
            grouped = tile(name + "_bf", [P, count * P * PACK], BF16)
            copy(
                out=grouped[:].bitcast(F32).rearrange("s (c e u) -> s c e u", c=count, u=2),
                in_=turned[:].rearrange("s c u e -> s c e u"),
            )
            return grouped[:]

        ut_mx = weights("ut", r_exp, r_sum, 0, size4, "mem")
        wt_mx = weights("wt", p_exp, p_sum, 1, wf4, "win")
        gots = [gather_values(j) for j in range(BLOCKS)]
        acc = [ps.tile([P, P * len(blocks)], F32, name="acc%d" % n) for n, blocks in enumerate(WVAL_LOADS)]
        early_mx = mx_tiles("vt_early", 3 * P, "vals_raw3")
        quantize_into(early_mx, slice(0, 2 * P), values("vt01", (0, 1), "pair", nc.vector.tensor_copy))
        quantize_into(early_mx, slice(2 * P, 3 * P), values("vt2", (2,), "win", nc.scalar.copy))
        last_mx = quantize("vt_last", values("vt3", (3,), "mem", nc.scalar.copy), P)
        product(acc[2][:], ut_mx, early_mx, slice(0, P), True, False)
        product(acc[1][:], ut_mx, early_mx, slice(P, 2 * P), True, False)
        product(acc[0][:, :P], ut_mx, early_mx, slice(2 * P, 3 * P), True, False)
        product(acc[0][:, P:], ut_mx, last_mx, slice(0, P), False, False)

        for n, blocks in enumerate(WVAL_LOADS):
            width = P * len(blocks)
            grouped = tile("wval_bf%d" % n, [P, width, PACK], BF16)
            whole, low, high = slice(0, width), slice(0, width // 2), slice(width // 2, width)
            if n == 0:
                interleave(nc.vector.tensor_copy, grouped, wval_raw[n], (whole, whole))
            elif n == 1:
                interleave(nc.scalar.copy, grouped, wval_raw[n], (whole, whole))
            else:
                interleave(nc.vector.tensor_copy, grouped, wval_raw[n], (low, low))
                interleave(nc.scalar.copy, grouped, wval_raw[n], (high, high))
            wval_mx = quantize("wval%d" % n, grouped[:].rearrange("p e j -> p (e j)"), width)
            product(acc[n][:], wt_mx, wval_mx, slice(0, width), False, True)
            result = tile("result%d" % n, [P, width], F32)
            nc.scalar.copy(out=result[:], in_=acc[n][:])
            nc.sync.dma_start(out=out[:, blocks[0] * P : (blocks[-1] + 1) * P], in_=result[:])
